import numpy as np
import ml_dtypes

BF16 = ml_dtypes.bfloat16


def bf(x):
    return np.asarray(x, np.float32).astype(BF16)


def f32(x):
    return np.asarray(x, np.float32)


def f64(x):
    return np.asarray(x).astype(np.float64)


def striped(idx):
    return np.tile(idx.reshape(-1, 16).T, (8, 1))


S, K, M, N, V = 1024, 256, 256, 256, 128


def setup_inputs():
    return {"table": bf(np.random.standard_normal((K, S))), "w": bf(np.random.standard_normal((K, M)) / np.sqrt(K)), "s": f32(0.5 + np.random.random_sample((M, 1))), "offs": striped(np.random.permutation(S)[:N])}


def reference(table, w, s, offs):
    idx = offs[:16].T.reshape(-1)
    x = f64(table)[:, idx]
    p = f64(w).T @ x[:, :V]
    q = f64(w).T @ x[:, V:]
    return (p - q) ** 2 * f64(s)

@@ -1,0 +1,56 @@
+import concourse.mybir as mybir
+
+P = 128
+S, K, M, V = 1024, 256, 256, 128
+N = 2 * V
+LIST_ROWS = 16
+FLOPS = 2 * K * M * N
+
+BF16, F32, U16 = mybir.dt.bfloat16, mybir.dt.float32, mybir.dt.uint16
+MULT = mybir.AluOpType.mult
+
+
+def tile_rows_pair_sqd_sub_kernel(tc, table, w, s, offs, out):
+    nc = tc.nc
+    k_blocks, m_blocks = K // P, M // P
+    with (
+        tc.tile_pool(name="held", bufs=1) as held,
+        tc.psum_pool(name="psum", bufs=1) as psum,
+    ):
+        table_rows = table.rearrange("(p a) n -> a p n", a=k_blocks)
+        windows = [held.tile([P, S], BF16, name=f"window{a}") for a in range(k_blocks)]
+        offsets = held.tile([P, N // LIST_ROWS], U16, name="offsets")
+        w_plus = held.tile([P, k_blocks * M], BF16, name="w_plus")
+        w_minus = held.tile([P, k_blocks * M], BF16, name="w_minus")
+        gain = held.tile([P, m_blocks], F32, name="gain")
+
+        nc.sync.dma_start(windows[0][:], table_rows[0])
+        nc.sync.dma_start(offsets[:], offs)
+        nc.sync.dma_start(windows[1][:], table_rows[1])
+        nc.scalar.dma_start(w_plus[:], w.rearrange("(p a) m -> p (a m)", a=k_blocks))
+        nc.scalar.dma_start(gain[:], s.rearrange("(b p) o -> p (b o)", p=P))
+
+        nc.vector.tensor_scalar_mul(w_minus[:], w_plus[:], -1.0)
+
+        half = V // LIST_ROWS
+        sides = ((w_plus, offsets[:, :half]), (w_minus, offsets[:, half:]))
+        diffs = [psum.tile([P, V], F32, name=f"diff{b}") for b in range(m_blocks)]
+        for a in range(k_blocks):
+            for b in range(m_blocks):
+                for side, (weights, picked) in enumerate(sides):
+                    column = a * M + b * P
+                    nc.tensor.matmul(
+                        diffs[b][:],
+                        weights[:, column : column + P],
+                        windows[a][:].indirect(picked),
+                        start=(a == 0 and side == 0),
+                        stop=(a == k_blocks - 1 and side == len(sides) - 1),
+                    )
+
+        store_queues = (nc.scalar, nc.sync)
+        for b in range(m_blocks):
+            scaled = held.tile([P, V], F32, name=f"scaled{b}")
+            result = held.tile([P, V], F32, name=f"result{b}")
+            nc.vector.tensor_scalar_mul(scaled[:], diffs[b][:], gain[:, b : b + 1])
+            nc.vector.tensor_tensor(result[:], diffs[b][:], scaled[:], MULT)
+            store_queues[b].dma_start(out[b * P : (b + 1) * P, :], result[:])

@@ -7,7 +7,7 @@ LIST_ROWS = 16
 FLOPS = 2 * K * M * N
 
 BF16, F32, U16 = mybir.dt.bfloat16, mybir.dt.float32, mybir.dt.uint16
-MULT = mybir.AluOpType.mult
+SQUARE = mybir.ActivationFunctionType.Square
 
 
 def tile_rows_pair_sqd_sub_kernel(tc, table, w, s, offs, out):
@@ -30,6 +30,11 @@ def tile_rows_pair_sqd_sub_kernel(tc, table, w, s, offs, out):
         nc.scalar.dma_start(w_plus[:], w.rearrange("(p a) m -> p (a m)", a=k_blocks))
         nc.scalar.dma_start(gain[:], s.rearrange("(b p) o -> p (b o)", p=P))
 
+        zeros = held.tile([P, 1], F32, name="zeros")
+        warm = held.tile([P, 1], F32, name="warm")
+        nc.vector.memset(zeros[:], 0.0)
+        nc.scalar.activation(warm[:], zeros[:], SQUARE)
+
         nc.vector.tensor_scalar_mul(w_minus[:], w_plus[:], -1.0)
 
         half = V // LIST_ROWS
@@ -47,10 +52,9 @@ def tile_rows_pair_sqd_sub_kernel(tc, table, w, s, offs, out):
                         stop=(a == k_blocks - 1 and side == len(sides) - 1),
                     )
 
-        store_queues = (nc.scalar, nc.sync)
         for b in range(m_blocks):
-            scaled = held.tile([P, V], F32, name=f"scaled{b}")
+            squared = held.tile([P, V], F32, name=f"squared{b}")
             result = held.tile([P, V], F32, name=f"result{b}")
-            nc.vector.tensor_scalar_mul(scaled[:], diffs[b][:], gain[:, b : b + 1])
-            nc.vector.tensor_tensor(result[:], diffs[b][:], scaled[:], MULT)
-            store_queues[b].dma_start(out[b * P : (b + 1) * P, :], result[:])
+            nc.scalar.activation(squared[:], diffs[b][:], SQUARE)
+            nc.vector.tensor_scalar_mul(result[:], squared[:], gain[:, b : b + 1])
+            nc.sync.dma_start(out[b * P : (b + 1) * P, :], result[:])

@@ -24,10 +24,10 @@ def tile_rows_pair_sqd_sub_kernel(tc, table, w, s, offs, out):
         w_minus = held.tile([P, k_blocks * M], BF16, name="w_minus")
         gain = held.tile([P, m_blocks], F32, name="gain")
 
-        nc.sync.dma_start(windows[0][:], table_rows[0])
         nc.sync.dma_start(offsets[:], offs)
-        nc.sync.dma_start(windows[1][:], table_rows[1])
-        nc.scalar.dma_start(w_plus[:], w.rearrange("(p a) m -> p (a m)", a=k_blocks))
+        nc.sync.dma_start(w_plus[:], w.rearrange("(p a) m -> p (a m)", a=k_blocks))
+        for a in range(k_blocks):
+            nc.scalar.dma_start(windows[a][:], table_rows[a])
         nc.scalar.dma_start(gain[:], s.rearrange("(b p) o -> p (b o)", p=P))
 
         zeros = held.tile([P, 1], F32, name="zeros")
@@ -38,19 +38,22 @@ def tile_rows_pair_sqd_sub_kernel(tc, table, w, s, offs, out):
         nc.vector.tensor_scalar_mul(w_minus[:], w_plus[:], -1.0)
 
         half = V // LIST_ROWS
-        sides = ((w_plus, offsets[:, :half]), (w_minus, offsets[:, half:]))
+        firsts, seconds = offsets[:, :half], offsets[:, half:]
         diffs = [psum.tile([P, V], F32, name=f"diff{b}") for b in range(m_blocks)]
-        for a in range(k_blocks):
-            for b in range(m_blocks):
-                for side, (weights, picked) in enumerate(sides):
-                    column = a * M + b * P
-                    nc.tensor.matmul(
-                        diffs[b][:],
-                        weights[:, column : column + P],
-                        windows[a][:].indirect(picked),
-                        start=(a == 0 and side == 0),
-                        stop=(a == k_blocks - 1 and side == len(sides) - 1),
-                    )
+
+        def project(a, b, weights, picked, start=False, stop=False):
+            column = a * M + b * P
+            nc.tensor.matmul(
+                diffs[b][:], weights[:, column : column + P], windows[a][:].indirect(picked), start=start, stop=stop
+            )
+
+        for b in range(m_blocks):
+            project(0, b, w_plus, firsts, start=True)
+        for b in range(m_blocks):
+            project(0, b, w_minus, seconds)
+        for b in range(m_blocks):
+            project(1, b, w_plus, firsts)
+            project(1, b, w_minus, seconds, stop=True)
 
         for b in range(m_blocks):
             squared = held.tile([P, V], F32, name=f"squared{b}")

@@ -17,17 +17,17 @@ def tile_rows_pair_sqd_sub_kernel(tc, table, w, s, offs, out):
         tc.tile_pool(name="held", bufs=1) as held,
         tc.psum_pool(name="psum", bufs=1) as psum,
     ):
-        table_rows = table.rearrange("(p a) n -> a p n", a=k_blocks)
         windows = [held.tile([P, S], BF16, name=f"window{a}") for a in range(k_blocks)]
+        w_plus = [held.tile([P, M], BF16, name=f"w_plus{a}") for a in range(k_blocks)]
+        w_minus = [held.tile([P, M], BF16, name=f"w_minus{a}") for a in range(k_blocks)]
         offsets = held.tile([P, N // LIST_ROWS], U16, name="offsets")
-        w_plus = held.tile([P, k_blocks * M], BF16, name="w_plus")
-        w_minus = held.tile([P, k_blocks * M], BF16, name="w_minus")
         gain = held.tile([P, m_blocks], F32, name="gain")
 
         nc.sync.dma_start(offsets[:], offs)
-        nc.sync.dma_start(w_plus[:], w.rearrange("(p a) m -> p (a m)", a=k_blocks))
-        for a in range(k_blocks):
-            nc.scalar.dma_start(windows[a][:], table_rows[a])
+        nc.sync.dma_start(w_plus[0][:], w[:P, :])
+        nc.scalar.dma_start(windows[0][:], table[:P, :])
+        nc.scalar.dma_start(w_plus[1][:], w[P:, :])
+        nc.scalar.dma_start(windows[1][:], table[P:, :])
         nc.scalar.dma_start(gain[:], s.rearrange("(b p) o -> p (b o)", p=P))
 
         zeros = held.tile([P, 1], F32, name="zeros")
@@ -35,16 +35,16 @@ def tile_rows_pair_sqd_sub_kernel(tc, table, w, s, offs, out):
         nc.vector.memset(zeros[:], 0.0)
         nc.scalar.activation(warm[:], zeros[:], SQUARE)
 
-        nc.vector.tensor_scalar_mul(w_minus[:], w_plus[:], -1.0)
+        for a in range(k_blocks):
+            nc.vector.tensor_scalar_mul(w_minus[a][:], w_plus[a][:], -1.0)
 
         half = V // LIST_ROWS
         firsts, seconds = offsets[:, :half], offsets[:, half:]
         diffs = [psum.tile([P, V], F32, name=f"diff{b}") for b in range(m_blocks)]
 
         def project(a, b, weights, picked, start=False, stop=False):
-            column = a * M + b * P
             nc.tensor.matmul(
-                diffs[b][:], weights[:, column : column + P], windows[a][:].indirect(picked), start=start, stop=stop
+                diffs[b][:], weights[a][:, b * P : (b + 1) * P], windows[a][:].indirect(picked), start=start, stop=stop
             )
 
         for b in range(m_blocks):

import concourse.mybir as mybir

P = 128
S, K, M, V = 1024, 256, 256, 128
N = 2 * V
LIST_ROWS = 16
FLOPS = 2 * K * M * N

BF16, F32, U16 = mybir.dt.bfloat16, mybir.dt.float32, mybir.dt.uint16
SQUARE = mybir.ActivationFunctionType.Square


def tile_rows_pair_sqd_sub_kernel(tc, table, w, s, offs, out):
    nc = tc.nc
    k_blocks, m_blocks = K // P, M // P
    with (
        tc.tile_pool(name="held", bufs=1) as held,
        tc.psum_pool(name="psum", bufs=1) as psum,
    ):
        windows = [held.tile([P, S], BF16, name=f"window{a}") for a in range(k_blocks)]
        w_plus = [held.tile([P, M], BF16, name=f"w_plus{a}") for a in range(k_blocks)]
        w_minus = [held.tile([P, M], BF16, name=f"w_minus{a}") for a in range(k_blocks)]
        offsets = held.tile([P, N // LIST_ROWS], U16, name="offsets")
        gain = held.tile([P, m_blocks], F32, name="gain")

        nc.sync.dma_start(offsets[:], offs)
        nc.sync.dma_start(w_plus[0][:], w[:P, :])
        nc.scalar.dma_start(windows[0][:], table[:P, :])
        nc.scalar.dma_start(w_plus[1][:], w[P:, :])
        nc.scalar.dma_start(windows[1][:], table[P:, :])
        nc.scalar.dma_start(gain[:], s.rearrange("(b p) o -> p (b o)", p=P))

        zeros = held.tile([P, 1], F32, name="zeros")
        warm = held.tile([P, 1], F32, name="warm")
        nc.vector.memset(zeros[:], 0.0)
        nc.scalar.activation(warm[:], zeros[:], SQUARE)

        for a in range(k_blocks):
            nc.vector.tensor_scalar_mul(w_minus[a][:], w_plus[a][:], -1.0)

        half = V // LIST_ROWS
        firsts, seconds = offsets[:, :half], offsets[:, half:]
        diffs = [psum.tile([P, V], F32, name=f"diff{b}") for b in range(m_blocks)]

        def project(a, b, weights, picked, start=False, stop=False):
            nc.tensor.matmul(
                diffs[b][:], weights[a][:, b * P : (b + 1) * P], windows[a][:].indirect(picked), start=start, stop=stop
            )

        for b in range(m_blocks):
            project(0, b, w_plus, firsts, start=True)
        for b in range(m_blocks):
            project(0, b, w_minus, seconds)
        for b in range(m_blocks):
            project(1, b, w_plus, firsts)
            project(1, b, w_minus, seconds, stop=True)

        for b in range(m_blocks):
            squared = held.tile([P, V], F32, name=f"squared{b}")
            result = held.tile([P, V], F32, name=f"result{b}")
            nc.scalar.activation(squared[:], diffs[b][:], SQUARE)
            nc.vector.tensor_scalar_mul(result[:], squared[:], gain[:, b : b + 1])
            nc.sync.dma_start(out[b * P : (b + 1) * P, :], result[:])
